import numpy as np
import ml_dtypes


def mxq(x, axis, fmt="e4m3"):
    dtype, down = {"e4m3": (ml_dtypes.float8_e4m3fn, 7), "e5m2": (ml_dtypes.float8_e5m2, 14)}[fmt]
    v = np.moveaxis(np.asarray(x, np.float32).astype(ml_dtypes.bfloat16).astype(np.float64), axis, -1)
    blocks = v.reshape(v.shape[:-1] + (-1, 32))
    amax = np.abs(blocks).max(-1, keepdims=True)
    byte = np.maximum(np.where(amax > 0, np.frexp(amax)[1] - 1 + 127, 0) - down, 1)
    scale = np.exp2(byte - 127.0)
    codes = (blocks / scale).astype(np.float32).astype(dtype).astype(np.float64)
    return np.moveaxis((codes * scale).reshape(v.shape), -1, axis)


WIDE = False


def mx_kscale(k):
    if not WIDE:
        return np.ones(k)
    levels = np.array([10, -10, 5, -5, 0])
    if k % 512:
        return np.exp2(np.random.permutation(np.resize(levels, k // 32))).repeat(32)
    a = np.empty((k // 512, 16))
    for p in range(k // 512):
        a[p, :8] = np.random.permutation(np.resize(levels, 8))
        for g in range(8):
            far = levels[np.abs(levels - a[p, g]) >= 10]
            a[p, g + 8] = far[np.random.randint(len(far))]
    return np.exp2(a.ravel()).repeat(32)


def f64(x):
    return np.asarray(x).astype(np.float64)


def striped(idx):
    return np.tile(idx.reshape(-1, 16).T, (8, 1)).astype(np.uint16)


def unstriped(offs):
    return offs[:16].T.reshape(-1).astype(np.int64)


def pack_weight(w):
    k, n = w.shape
    w = f64(np.asarray(w, np.float32).astype(ml_dtypes.bfloat16)).reshape(k // 32, 32, n)
    amax = np.abs(w).max(1)
    byte = np.clip(np.where(amax > 0, np.frexp(amax)[1] - 1 + 127 - 7, 1), 1, 254)
    scaled = (w * np.exp2(127.0 - byte)[:, None, :]).reshape(k, n).astype(np.float32)
    words = np.ascontiguousarray(scaled.reshape(k // 512, 128, 4, n).transpose(0, 1, 3, 2)).astype(ml_dtypes.float8_e4m3fn).view(np.uint8)
    return words, np.ascontiguousarray(byte.astype(np.uint8).reshape(k // 512, 16, n))


def unpack_weight(words, scales):
    g, p, n, _ = words.shape
    vals = np.ascontiguousarray(words).view(ml_dtypes.float8_e4m3fn).astype(np.float64) * np.repeat(np.exp2(scales.astype(np.float64) - 127.0), 8, axis=1)[..., None]
    return vals.transpose(0, 1, 3, 2).reshape(g * 512, n)


def planes(y):
    n, m = y.shape
    v = y.astype(np.float32).astype(ml_dtypes.bfloat16).astype(np.float64).reshape(n // 32, 32, m)
    top = np.abs(v).max(1)
    byte = np.clip(np.where(top > 0, np.frexp(top)[1] - 1 + 127 - 7, 1), 1, 254)
    codes = (v * np.exp2(127.0 - byte)[:, None, :]).reshape(n, m).astype(np.float32).astype(ml_dtypes.float8_e4m3fn).view(np.uint8)
    words = codes.reshape(n // 512, 128, 4, m).transpose(0, 1, 3, 2)
    return np.ascontiguousarray(words), np.ascontiguousarray(byte.astype(np.uint8).reshape(n // 512, 16, m))


def gelu(v):
    return 0.5 * v * (1.0 + np.tanh(np.sqrt(2.0 / np.pi) * (v + 0.044715 * v**3)))


K, T, S, D, V, H, N = 512, 4096, 1024, 4, 256, 512, 512
P = 2 ** 7


def setup_inputs():
    n = np.random.standard_normal
    s = mx_kscale(K)[:, None]
    u = mx_kscale(H)
    packed_xT = pack_weight(n((K, T)) * s)
    packed_w2 = pack_weight(n((H, N)) / np.sqrt(H) / u[:, None])
    return {
        "x_words": packed_xT[0],
        "x_scales": packed_xT[1],
        "w1": (n((K, H)) / np.sqrt(K) / s * u).astype(np.float32),
        "w2_words": packed_w2[0],
        "w2_scales": packed_w2[1],
        "gate": (np.tile(np.random.uniform(0.2, 1.0, (D, 1, V)), (1, P, 1))).astype(np.float32),
        "offs": striped(np.random.permutation(T)[:S]),
    }


def reference(x_words, x_scales, w1, w2_words, w2_scales, gate, offs):
    xq = unpack_weight(x_words, x_scales)[:, unstriped(offs)]
    w1q = mxq(f64(w1), 0, "e4m3")
    y0 = w1q.T @ xq[:, :V]
    y1 = w1q.T @ xq[:, V:2 * V]
    y2 = w1q.T @ xq[:, 2 * V:3 * V]
    y3 = w1q.T @ xq[:, 3 * V:4 * V]
    z = gelu(y0 * f64(gate)[0, :1] + y1 * f64(gate)[1, :1] + y2 * f64(gate)[2, :1] + y3 * f64(gate)[3, :1])
    out_0 = unpack_weight(w2_words, w2_scales).T @ mxq(z, 0, "e4m3")
    return (out_0,) + planes(out_0)

@@ -1,0 +1,227 @@
+from contextlib import ExitStack
+
+import concourse.mybir as mybir
+from concourse.masks import make_identity
+
+K, T, S, D, V, H, N = 512, 4096, 1024, 4, 256, 512, 512
+FLOPS = 2 * K * H * S + 2 * H * N * V
+
+F32 = mybir.dt.float32
+BF16 = mybir.dt.bfloat16
+I32 = mybir.dt.int32
+U32 = mybir.dt.uint32
+U16 = mybir.dt.uint16
+U8 = mybir.dt.uint8
+FP8X4 = mybir.dt.float8_e4m3fn_x4
+ACT = mybir.ActivationFunctionType
+ALU = mybir.AluOpType
+
+P = 128
+PACK = 4
+HALVES = V // P
+SCALE_ROWS = 16
+PIECES = ((0, 128), (128, 192), (192, 256))
+STAGE_ROW = P - SCALE_ROWS
+
+
+def tile_picked_zbloom_gelu_po_kernel(
+    tc, x_words, x_scales, w1, w2_words, w2_scales, gate, offs, out_0, out_1, out_2
+):
+    nc = tc.nc
+    with ExitStack() as ctx:
+        keep = ctx.enter_context(tc.tile_pool(name="keep", bufs=1))
+        ybank = ctx.enter_context(tc.psum_pool(name="ybank", bufs=6))
+        ubank = ctx.enter_context(tc.psum_pool(name="ubank", bufs=2))
+
+        offsets = keep.tile([P, S // 16], U16, name="offsets")
+        nc.sync.dma_start(offsets[:], offs)
+
+        xs_table = keep.tile([P, T], U8, name="xs_table", align_bytes=64)
+        nc.sync.dma_start(
+            xs_table[STAGE_ROW : STAGE_ROW + SCALE_ROWS, :].bitcast(I32), x_scales[0].bitcast(I32)
+        )
+        nc.vector.memset(xs_table[0:STAGE_ROW, :].bitcast(I32), 0)
+
+        gate_rows = keep.tile([P, V], F32, name="gate_rows")
+        nc.sync.dma_start(gate_rows[P - D : P, :], gate[:, 0, :])
+        nc.vector.memset(gate_rows[0 : P - D, :], 0.0)
+
+        w1_raw = keep.tile([P, PACK, H], F32, name="w1_raw")
+        nc.sync.dma_start(w1_raw[:], w1.rearrange("(p j) c -> p j c", j=PACK))
+
+        xw_table = keep.tile([P, T], U32, name="xw_table", align_bytes=64)
+        nc.sync.dma_start(
+            xw_table[:].bitcast(I32), x_words[0].rearrange("p c r -> p (c r)").bitcast(I32)
+        )
+
+        w2w_raw = keep.tile([P, N], U32, name="w2w_raw", align_bytes=64)
+        nc.sync.dma_start(
+            w2w_raw[:].bitcast(I32), w2_words[0].rearrange("p c r -> p (c r)").bitcast(I32)
+        )
+
+        ident = keep.tile([P, P], F32, name="ident")
+        make_identity(nc, ident[:])
+
+        w2s_raw = keep.tile([P, N], U8, name="w2s_raw", align_bytes=64)
+        nc.gpsimd.memset(w2s_raw[:].bitcast(I32), 0)
+        for q in range(4):
+            nc.gpsimd.dma_start(
+                w2s_raw[32 * q : 32 * q + 4, :].bitcast(I32),
+                w2_scales[0, 4 * q : 4 * q + 4, :].bitcast(I32),
+            )
+
+        xs_plane = keep.tile([P, S], U8, name="xs_plane", align_bytes=64)
+        nc.vector.memset(xs_plane[:].bitcast(I32), 0)
+
+        gate_t = ubank.tile([P, HALVES, P], F32, name="gate_t", tag="u")
+        for h in range(HALVES):
+            nc.tensor.transpose(gate_t[:, h, :], gate_rows[:, h * P : (h + 1) * P], ident[:])
+        gcol = keep.tile([P, HALVES, D], F32, name="gcol")
+        nc.scalar.copy(gcol[:], gate_t[:, :, P - D : P])
+
+        xs_picked = keep.tile([P, S], U8, name="xs_picked", align_bytes=64)
+        nc.vector.tensor_copy(xs_picked[:], xs_table[:].indirect(offsets[:]))
+        for q in range(4):
+            nc.scalar.dma_start(
+                xs_plane[32 * q : 32 * q + 4, :].bitcast(I32),
+                xs_picked[STAGE_ROW + 4 * q : STAGE_ROW + 4 * q + 4, :].bitcast(I32),
+            )
+
+        w1_bf = keep.tile([P, PACK * H], BF16, name="w1_bf", align_bytes=64)
+        nc.vector.tensor_copy(
+            w1_bf[:].rearrange("p (t m j) -> p m j t", t=PACK, j=PACK),
+            w1_raw[:].rearrange("p j (m t) -> p m j t", t=PACK),
+        )
+        w1_codes = keep.tile([P, H], U32, name="w1_codes", align_bytes=64)
+        w1_plane = keep.tile([P, H], U8, name="w1_plane", align_bytes=64)
+        nc.vector.quantize_mx(out=w1_codes[:].bitcast(FP8X4), scales=w1_plane[:], in_=w1_bf[:])
+
+        w2_codes = keep.tile([P, N], U32, name="w2_codes", align_bytes=64)
+        nc.scalar.copy(
+            w2_codes[:].rearrange("p (t m) -> p m t", t=PACK),
+            w2w_raw[:].rearrange("p (m t) -> p m t", t=PACK),
+        )
+
+        xw_picked = []
+        for d in range(D):
+            picked = keep.tile([P, V], U32, name="xw_picked%d" % d, align_bytes=64)
+            nc.vector.tensor_copy(
+                picked[:], xw_table[:].indirect(offsets[:, d * V // 16 : (d + 1) * V // 16])
+            )
+            xw_picked.append(picked)
+
+        def product(d, h):
+            y = ybank.tile([P, H], F32, name="y%d%d" % (d, h), tag="y")
+            nc.tensor.matmul_mx(
+                out=y[:],
+                lhsT=xw_picked[d][:, h * P : (h + 1) * P].bitcast(FP8X4),
+                lhsT_scale=xs_plane[:, d * V + h * P : d * V + (h + 1) * P],
+                rhs=w1_codes[:].bitcast(FP8X4),
+                rhs_scale=w1_plane[:],
+                start=True,
+                stop=True,
+            )
+            return y
+
+        def gated_on_scalar(d, h, tag):
+            y = product(d, h)
+            term = keep.tile([P, H], F32, name="term%d%d" % (d, h), tag=tag, align_bytes=64)
+            nc.scalar.activation(term[:], y[:], ACT.Copy, scale=gcol[:, h, d : d + 1])
+            return term
+
+        def gated_on_vector(d, h, tag):
+            y = product(d, h)
+            term = keep.tile([P, H], F32, name="term%d%d" % (d, h), tag=tag, align_bytes=64)
+            nc.vector.tensor_scalar_mul(term[:], y[:], gcol[:, h, d : d + 1])
+            return term
+
+        def gated_plus(d, h, other, tag):
+            y = product(d, h)
+            term = keep.tile([P, H], F32, name="term%d%d" % (d, h), tag=tag, align_bytes=64)
+            nc.vector.scalar_tensor_tensor(
+                term[:], y[:], gcol[:, h, d : d + 1], other[:], ALU.mult, ALU.add
+            )
+            return term
+
+        a0 = gated_on_scalar(0, 0, "a0")
+        b0 = gated_on_scalar(1, 0, "b")
+        c0 = gated_plus(2, 0, a0, "c0")
+        d0 = gated_plus(3, 0, b0, "d0")
+        a1 = gated_on_scalar(0, 1, "a1")
+        b1 = gated_on_vector(1, 1, "b")
+        c1 = gated_on_scalar(2, 1, "c1")
+        d1 = gated_plus(3, 1, a1, "d1")
+        w2_plane = keep.tile([P, N], U8, name="w2_plane", align_bytes=64, tag="a1")
+        nc.vector.tensor_copy(
+            w2_plane[:].rearrange("p (t m) -> p m t", t=PACK),
+            w2s_raw[:].rearrange("p (m t) -> p m t", t=PACK),
+        )
+        terms = [[c0, d0], [b1, c1, d1]]
+
+        out_codes = keep.tile([P, V], U32, name="out_codes", align_bytes=64)
+        out_plane = keep.tile([P, V], U8, name="out_plane", align_bytes=64)
+        out_rows = out_0.rearrange("(p t) v -> p t v", t=PACK)
+        out_words = out_1[0].rearrange("p c r -> p (c r)").bitcast(I32)
+
+        sums = []
+        for h in range(HALVES):
+            u = ubank.tile([P, PACK, P], F32, name="u%d" % h, tag="u")
+            steps = [(term, t) for term in terms[h] for t in range(PACK)]
+            for n, (term, t) in enumerate(steps):
+                nc.tensor.matmul(
+                    u[:, t, :],
+                    term[:, t * P : (t + 1) * P],
+                    ident[:],
+                    start=(n == 0),
+                    stop=(n == len(steps) - 1),
+                    is_transpose=True,
+                )
+            sums.append(u)
+
+        z_ops = []
+        for lo, hi in PIECES:
+            width = hi - lo
+            u = sums[lo // P]
+            z_bf = keep.tile([P, width * PACK], BF16, name="z_bf%d" % lo, align_bytes=64)
+            nc.scalar.activation(
+                z_bf[:].rearrange("p (v t) -> p v t", t=PACK),
+                u[:, :, lo % P : lo % P + width].rearrange("p t v -> p v t"),
+                ACT.Gelu_apprx_tanh,
+            )
+            z_codes = keep.tile([P, width], U32, name="z_codes%d" % lo, align_bytes=64)
+            z_plane = keep.tile([P, width], U8, name="z_plane%d" % lo, align_bytes=64)
+            nc.vector.quantize_mx(out=z_codes[:].bitcast(FP8X4), scales=z_plane[:], in_=z_bf[:])
+            z_ops.append((z_codes, z_plane))
+
+        for (lo, hi), (z_codes, z_plane) in zip(PIECES, z_ops):
+            width = hi - lo
+            cols = slice(lo, hi)
+            o = ybank.tile([P, PACK, width], F32, name="o%d" % lo, tag="y")
+            for t in range(PACK):
+                nc.tensor.matmul_mx(
+                    out=o[:, t, :],
+                    lhsT=w2_codes[:, t * P : (t + 1) * P].bitcast(FP8X4),
+                    lhsT_scale=w2_plane[:, t * P : (t + 1) * P],
+                    rhs=z_codes[:].bitcast(FP8X4),
+                    rhs_scale=z_plane[:],
+                    start=True,
+                    stop=True,
+                )
+            o_bf = keep.tile([P, width * PACK], BF16, name="o_bf%d" % lo, align_bytes=64)
+            nc.vector.tensor_copy(
+                o_bf[:].rearrange("p (v t) -> p v t", t=PACK), o[:].rearrange("p t v -> p v t")
+            )
+            o_f32 = keep.tile([P, PACK, width], F32, name="o_f32%d" % lo)
+            nc.scalar.copy(o_f32[:], o[:])
+            nc.sync.dma_start(out_rows[:, :, cols], o_f32[:])
+            nc.vector.quantize_mx(
+                out=out_codes[:, cols].bitcast(FP8X4), scales=out_plane[:, cols], in_=o_bf[:]
+            )
+
+        nc.sync.dma_start(out_words, out_codes[:].bitcast(I32))
+        for q in range(4):
+            queue = nc.scalar if q % 2 == 0 else nc.sync
+            queue.dma_start(
+                out_2[0, 4 * q : 4 * q + 4, :].bitcast(I32),
+                out_plane[32 * q : 32 * q + 4, :].bitcast(I32),
+            )

@@ -30,8 +30,7 @@ def tile_picked_zbloom_gelu_po_kernel(
     nc = tc.nc
     with ExitStack() as ctx:
         keep = ctx.enter_context(tc.tile_pool(name="keep", bufs=1))
-        ybank = ctx.enter_context(tc.psum_pool(name="ybank", bufs=6))
-        ubank = ctx.enter_context(tc.psum_pool(name="ubank", bufs=2))
+        psum = ctx.enter_context(tc.psum_pool(name="psum", bufs=1))
 
         offsets = keep.tile([P, S // 16], U16, name="offsets")
         nc.sync.dma_start(offsets[:], offs)
@@ -47,11 +46,13 @@ def tile_picked_zbloom_gelu_po_kernel(
         nc.vector.memset(gate_rows[0 : P - D, :], 0.0)
 
         w1_raw = keep.tile([P, PACK, H], F32, name="w1_raw")
-        nc.sync.dma_start(w1_raw[:], w1.rearrange("(p j) c -> p j c", j=PACK))
+        nc.sync.dma_start(w1_raw[:], w1.rearrange("(p j) c -> p j c", j=PACK), max_dma_last_dim=4096)
 
         xw_table = keep.tile([P, T], U32, name="xw_table", align_bytes=64)
         nc.sync.dma_start(
-            xw_table[:].bitcast(I32), x_words[0].rearrange("p c r -> p (c r)").bitcast(I32)
+            xw_table[:].bitcast(I32),
+            x_words[0].rearrange("p c r -> p (c r)").bitcast(I32),
+            max_dma_last_dim=4096,
         )
 
         w2w_raw = keep.tile([P, N], U32, name="w2w_raw", align_bytes=64)
@@ -73,7 +74,7 @@ def tile_picked_zbloom_gelu_po_kernel(
         xs_plane = keep.tile([P, S], U8, name="xs_plane", align_bytes=64)
         nc.vector.memset(xs_plane[:].bitcast(I32), 0)
 
-        gate_t = ubank.tile([P, HALVES, P], F32, name="gate_t", tag="u")
+        gate_t = psum.tile([P, HALVES, P], F32, name="gate_t", tag="bank7")
         for h in range(HALVES):
             nc.tensor.transpose(gate_t[:, h, :], gate_rows[:, h * P : (h + 1) * P], ident[:])
         gcol = keep.tile([P, HALVES, D], F32, name="gcol")
@@ -89,13 +90,18 @@ def tile_picked_zbloom_gelu_po_kernel(
 
         w1_bf = keep.tile([P, PACK * H], BF16, name="w1_bf", align_bytes=64)
         nc.vector.tensor_copy(
-            w1_bf[:].rearrange("p (t m j) -> p m j t", t=PACK, j=PACK),
-            w1_raw[:].rearrange("p j (m t) -> p m j t", t=PACK),
+            w1_bf[:].rearrange("p (c j) -> p c j", j=PACK),
+            w1_raw[:].rearrange("p j c -> p c j"),
         )
         w1_codes = keep.tile([P, H], U32, name="w1_codes", align_bytes=64)
         w1_plane = keep.tile([P, H], U8, name="w1_plane", align_bytes=64)
         nc.vector.quantize_mx(out=w1_codes[:].bitcast(FP8X4), scales=w1_plane[:], in_=w1_bf[:])
 
+        w2_plane = keep.tile([P, N], U8, name="w2_plane", align_bytes=64)
+        nc.gpsimd.tensor_copy(
+            w2_plane[:].rearrange("p (t m) -> p t m", t=PACK),
+            w2s_raw[:].rearrange("p (m t) -> p t m", t=PACK),
+        )
         w2_codes = keep.tile([P, N], U32, name="w2_codes", align_bytes=64)
         nc.scalar.copy(
             w2_codes[:].rearrange("p (t m) -> p m t", t=PACK),
@@ -111,7 +117,7 @@ def tile_picked_zbloom_gelu_po_kernel(
             xw_picked.append(picked)
 
         def product(d, h):
-            y = ybank.tile([P, H], F32, name="y%d%d" % (d, h), tag="y")
+            y = psum.tile([P, H], F32, name="y%d%d" % (d, h), tag="bank%d" % ((D * h + d) % 6))
             nc.tensor.matmul_mx(
                 out=y[:],
                 lhsT=xw_picked[d][:, h * P : (h + 1) * P].bitcast(FP8X4),
@@ -121,41 +127,43 @@ def tile_picked_zbloom_gelu_po_kernel(
                 start=True,
                 stop=True,
             )
-            return y
+            return y[:].rearrange("p (m t) -> p t m", t=PACK)
 
         def gated_on_scalar(d, h, tag):
             y = product(d, h)
-            term = keep.tile([P, H], F32, name="term%d%d" % (d, h), tag=tag, align_bytes=64)
-            nc.scalar.activation(term[:], y[:], ACT.Copy, scale=gcol[:, h, d : d + 1])
+            term = keep.tile([P, PACK, P], F32, name="term%d%d" % (d, h), tag=tag, align_bytes=64)
+            nc.scalar.activation(term[:], y, ACT.Copy, scale=gcol[:, h, d : d + 1])
             return term
 
         def gated_on_vector(d, h, tag):
             y = product(d, h)
-            term = keep.tile([P, H], F32, name="term%d%d" % (d, h), tag=tag, align_bytes=64)
-            nc.vector.tensor_scalar_mul(term[:], y[:], gcol[:, h, d : d + 1])
+            term = keep.tile([P, PACK, P], F32, name="term%d%d" % (d, h), tag=tag, align_bytes=64)
+            nc.vector.tensor_scalar_mul(term[:], y, gcol[:, h, d : d + 1])
             return term
 
-        def gated_plus(d, h, other, tag):
+        def gated_plus(d, h, other, tag, step):
             y = product(d, h)
-            term = keep.tile([P, H], F32, name="term%d%d" % (d, h), tag=tag, align_bytes=64)
-            nc.vector.scalar_tensor_tensor(
-                term[:], y[:], gcol[:, h, d : d + 1], other[:], ALU.mult, ALU.add
-            )
+            term = keep.tile([P, PACK, P], F32, name="term%d%d" % (d, h), tag=tag, align_bytes=64)
+            for t0 in range(0, PACK, step):
+                part = slice(t0, t0 + step)
+                nc.vector.scalar_tensor_tensor(
+                    term[:, part, :],
+                    y[:, part, :],
+                    gcol[:, h, d : d + 1],
+                    other[:, part, :],
+                    ALU.mult,
+                    ALU.add,
+                )
             return term
 
         a0 = gated_on_scalar(0, 0, "a0")
         b0 = gated_on_scalar(1, 0, "b")
-        c0 = gated_plus(2, 0, a0, "c0")
-        d0 = gated_plus(3, 0, b0, "d0")
+        c0 = gated_plus(2, 0, a0, "c0", PACK)
+        d0 = gated_plus(3, 0, b0, "d0", PACK)
         a1 = gated_on_scalar(0, 1, "a1")
         b1 = gated_on_vector(1, 1, "b")
         c1 = gated_on_scalar(2, 1, "c1")
-        d1 = gated_plus(3, 1, a1, "d1")
-        w2_plane = keep.tile([P, N], U8, name="w2_plane", align_bytes=64, tag="a1")
-        nc.vector.tensor_copy(
-            w2_plane[:].rearrange("p (t m) -> p m t", t=PACK),
-            w2s_raw[:].rearrange("p (m t) -> p m t", t=PACK),
-        )
+        d1 = gated_plus(3, 1, a1, "d1", PACK // 2)
         terms = [[c0, d0], [b1, c1, d1]]
 
         out_codes = keep.tile([P, V], U32, name="out_codes", align_bytes=64)
@@ -165,12 +173,12 @@ def tile_picked_zbloom_gelu_po_kernel(
 
         sums = []
         for h in range(HALVES):
-            u = ubank.tile([P, PACK, P], F32, name="u%d" % h, tag="u")
+            u = psum.tile([P, PACK, P], F32, name="u%d" % h, tag="bank%d" % (6 + h))
             steps = [(term, t) for term in terms[h] for t in range(PACK)]
             for n, (term, t) in enumerate(steps):
                 nc.tensor.matmul(
                     u[:, t, :],
-                    term[:, t * P : (t + 1) * P],
+                    term[:, t, :],
                     ident[:],
                     start=(n == 0),
                     stop=(n == len(steps) - 1),
@@ -193,10 +201,10 @@ def tile_picked_zbloom_gelu_po_kernel(
             nc.vector.quantize_mx(out=z_codes[:].bitcast(FP8X4), scales=z_plane[:], in_=z_bf[:])
             z_ops.append((z_codes, z_plane))
 
-        for (lo, hi), (z_codes, z_plane) in zip(PIECES, z_ops):
+        for n, ((lo, hi), (z_codes, z_plane)) in enumerate(zip(PIECES, z_ops)):
             width = hi - lo
             cols = slice(lo, hi)
-            o = ybank.tile([P, PACK, width], F32, name="o%d" % lo, tag="y")
+            o = psum.tile([P, PACK, width], F32, name="o%d" % lo, tag="bank%d" % (1 + n))
             for t in range(PACK):
                 nc.tensor.matmul_mx(
                     out=o[:, t, :],
@@ -213,7 +221,8 @@ def tile_picked_zbloom_gelu_po_kernel(
             )
             o_f32 = keep.tile([P, PACK, width], F32, name="o_f32%d" % lo)
             nc.scalar.copy(o_f32[:], o[:])
-            nc.sync.dma_start(out_rows[:, :, cols], o_f32[:])
+            queue = nc.scalar if hi == V else nc.sync
+            queue.dma_start(out_rows[:, :, cols], o_f32[:])
             nc.vector.quantize_mx(
                 out=out_codes[:, cols].bitcast(FP8X4), scales=out_plane[:, cols], in_=o_bf[:]
             )

@@ -20,7 +20,8 @@ P = 128
 PACK = 4
 HALVES = V // P
 SCALE_ROWS = 16
-PIECES = ((0, 128), (128, 192), (192, 256))
+PIECES = ((0, 128), (128, 256))
+ORDER = ((0, 0), (1, 0), (2, 0), (0, 1), (3, 0), (1, 1), (2, 1), (3, 1))
 STAGE_ROW = P - SCALE_ROWS
 
 
@@ -45,14 +46,13 @@ def tile_picked_zbloom_gelu_po_kernel(
         nc.sync.dma_start(gate_rows[P - D : P, :], gate[:, 0, :])
         nc.vector.memset(gate_rows[0 : P - D, :], 0.0)
 
-        w1_raw = keep.tile([P, PACK, H], F32, name="w1_raw")
-        nc.sync.dma_start(w1_raw[:], w1.rearrange("(p j) c -> p j c", j=PACK), max_dma_last_dim=4096)
+        w1_raw = keep.tile([P, PACK, H], F32, name="w1_raw", align_bytes=64, tag="w1_raw")
+        nc.sync.dma_start(w1_raw[:], w1.rearrange("(p j) c -> p j c", j=PACK))
 
         xw_table = keep.tile([P, T], U32, name="xw_table", align_bytes=64)
         nc.sync.dma_start(
             xw_table[:].bitcast(I32),
             x_words[0].rearrange("p c r -> p (c r)").bitcast(I32),
-            max_dma_last_dim=4096,
         )
 
         w2w_raw = keep.tile([P, N], U32, name="w2w_raw", align_bytes=64)
@@ -62,14 +62,6 @@ def tile_picked_zbloom_gelu_po_kernel(
 
         ident = keep.tile([P, P], F32, name="ident")
         make_identity(nc, ident[:])
-
-        w2s_raw = keep.tile([P, N], U8, name="w2s_raw", align_bytes=64)
-        nc.gpsimd.memset(w2s_raw[:].bitcast(I32), 0)
-        for q in range(4):
-            nc.gpsimd.dma_start(
-                w2s_raw[32 * q : 32 * q + 4, :].bitcast(I32),
-                w2_scales[0, 4 * q : 4 * q + 4, :].bitcast(I32),
-            )
 
         xs_plane = keep.tile([P, S], U8, name="xs_plane", align_bytes=64)
         nc.vector.memset(xs_plane[:].bitcast(I32), 0)
@@ -97,11 +89,14 @@ def tile_picked_zbloom_gelu_po_kernel(
         w1_plane = keep.tile([P, H], U8, name="w1_plane", align_bytes=64)
         nc.vector.quantize_mx(out=w1_codes[:].bitcast(FP8X4), scales=w1_plane[:], in_=w1_bf[:])
 
-        w2_plane = keep.tile([P, N], U8, name="w2_plane", align_bytes=64)
-        nc.gpsimd.tensor_copy(
-            w2_plane[:].rearrange("p (t m) -> p t m", t=PACK),
-            w2s_raw[:].rearrange("p (m t) -> p t m", t=PACK),
-        )
+        w2s_raw = keep.tile([P, N], U8, name="w2s_raw", align_bytes=64, tag="w1_raw")
+        nc.vector.memset(w2s_raw[:].bitcast(I32), 0)
+        for q in range(4):
+            nc.sync.dma_start(
+                w2s_raw[32 * q : 32 * q + 4, :].bitcast(I32),
+                w2_scales[0, 4 * q : 4 * q + 4, :].bitcast(I32),
+            )
+
         w2_codes = keep.tile([P, N], U32, name="w2_codes", align_bytes=64)
         nc.scalar.copy(
             w2_codes[:].rearrange("p (t m) -> p m t", t=PACK),
@@ -117,7 +112,7 @@ def tile_picked_zbloom_gelu_po_kernel(
             xw_picked.append(picked)
 
         def product(d, h):
-            y = psum.tile([P, H], F32, name="y%d%d" % (d, h), tag="bank%d" % ((D * h + d) % 6))
+            y = psum.tile([P, H], F32, name="y%d%d" % (d, h), tag="bank%d" % (ORDER.index((d, h)) % 6))
             nc.tensor.matmul_mx(
                 out=y[:],
                 lhsT=xw_picked[d][:, h * P : (h + 1) * P].bitcast(FP8X4),
@@ -133,12 +128,6 @@ def tile_picked_zbloom_gelu_po_kernel(
             y = product(d, h)
             term = keep.tile([P, PACK, P], F32, name="term%d%d" % (d, h), tag=tag, align_bytes=64)
             nc.scalar.activation(term[:], y, ACT.Copy, scale=gcol[:, h, d : d + 1])
-            return term
-
-        def gated_on_vector(d, h, tag):
-            y = product(d, h)
-            term = keep.tile([P, PACK, P], F32, name="term%d%d" % (d, h), tag=tag, align_bytes=64)
-            nc.vector.tensor_scalar_mul(term[:], y, gcol[:, h, d : d + 1])
             return term
 
         def gated_plus(d, h, other, tag, step):
@@ -157,14 +146,20 @@ def tile_picked_zbloom_gelu_po_kernel(
             return term
 
         a0 = gated_on_scalar(0, 0, "a0")
-        b0 = gated_on_scalar(1, 0, "b")
+        b0 = gated_on_scalar(1, 0, "b0")
         c0 = gated_plus(2, 0, a0, "c0", PACK)
-        d0 = gated_plus(3, 0, b0, "d0", PACK)
         a1 = gated_on_scalar(0, 1, "a1")
-        b1 = gated_on_vector(1, 1, "b")
-        c1 = gated_on_scalar(2, 1, "c1")
-        d1 = gated_plus(3, 1, a1, "d1", PACK // 2)
-        terms = [[c0, d0], [b1, c1, d1]]
+        d0 = gated_plus(3, 0, b0, "d0", PACK)
+        b1 = gated_on_scalar(1, 1, "b1")
+        c1 = gated_plus(2, 1, a1, "c1", PACK)
+        d1 = gated_plus(3, 1, b1, "d1", PACK // 2)
+        terms = [[c0, d0], [c1, d1]]
+
+        w2_plane = keep.tile([P, N], U8, name="w2_plane", align_bytes=64, tag="b1")
+        nc.vector.tensor_copy(
+            w2_plane[:].rearrange("p (t m) -> p t m", t=PACK),
+            w2s_raw[:].rearrange("p (m t) -> p t m", t=PACK),
+        )
 
         out_codes = keep.tile([P, V], U32, name="out_codes", align_bytes=64)
         out_plane = keep.tile([P, V], U8, name="out_plane", align_bytes=64)

@@ -66,6 +66,11 @@ def tile_picked_zbloom_gelu_po_kernel(
         xs_plane = keep.tile([P, S], U8, name="xs_plane", align_bytes=64)
         nc.vector.memset(xs_plane[:].bitcast(I32), 0)
 
+        seed = keep.tile([P, 1], F32, name="seed")
+        nc.vector.memset(seed[:], 0.0)
+        unread = keep.tile([P, 1], F32, name="unread")
+        nc.scalar.activation(unread[:], seed[:], ACT.Gelu_apprx_tanh)
+
         gate_t = psum.tile([P, HALVES, P], F32, name="gate_t", tag="bank7")
         for h in range(HALVES):
             nc.tensor.transpose(gate_t[:, h, :], gate_rows[:, h * P : (h + 1) * P], ident[:])

@@ -21,7 +21,7 @@ PACK = 4
 HALVES = V // P
 SCALE_ROWS = 16
 PIECES = ((0, 128), (128, 256))
-ORDER = ((0, 0), (1, 0), (2, 0), (0, 1), (3, 0), (1, 1), (2, 1), (3, 1))
+ORDER = ((0, 0), (0, 1), (1, 0), (1, 1), (2, 0), (3, 0), (2, 1), (3, 1))
 STAGE_ROW = P - SCALE_ROWS
 
 
@@ -37,13 +37,13 @@ def tile_picked_zbloom_gelu_po_kernel(
         nc.sync.dma_start(offsets[:], offs)
 
         xs_table = keep.tile([P, T], U8, name="xs_table", align_bytes=64)
-        nc.sync.dma_start(
+        nc.scalar.dma_start(
             xs_table[STAGE_ROW : STAGE_ROW + SCALE_ROWS, :].bitcast(I32), x_scales[0].bitcast(I32)
         )
         nc.vector.memset(xs_table[0:STAGE_ROW, :].bitcast(I32), 0)
 
         gate_rows = keep.tile([P, V], F32, name="gate_rows")
-        nc.sync.dma_start(gate_rows[P - D : P, :], gate[:, 0, :])
+        nc.scalar.dma_start(gate_rows[P - D : P, :], gate[:, 0, :])
         nc.vector.memset(gate_rows[0 : P - D, :], 0.0)
 
         w1_raw = keep.tile([P, PACK, H], F32, name="w1_raw", align_bytes=64, tag="w1_raw")
@@ -102,12 +102,6 @@ def tile_picked_zbloom_gelu_po_kernel(
                 w2_scales[0, 4 * q : 4 * q + 4, :].bitcast(I32),
             )
 
-        w2_codes = keep.tile([P, N], U32, name="w2_codes", align_bytes=64)
-        nc.scalar.copy(
-            w2_codes[:].rearrange("p (t m) -> p m t", t=PACK),
-            w2w_raw[:].rearrange("p (m t) -> p m t", t=PACK),
-        )
-
         xw_picked = []
         for d in range(D):
             picked = keep.tile([P, V], U32, name="xw_picked%d" % d, align_bytes=64)
@@ -129,10 +123,14 @@ def tile_picked_zbloom_gelu_po_kernel(
             )
             return y[:].rearrange("p (m t) -> p t m", t=PACK)
 
-        def gated_on_scalar(d, h, tag):
+        def gated_on_scalar(d, h, tag, step):
             y = product(d, h)
             term = keep.tile([P, PACK, P], F32, name="term%d%d" % (d, h), tag=tag, align_bytes=64)
-            nc.scalar.activation(term[:], y, ACT.Copy, scale=gcol[:, h, d : d + 1])
+            for t0 in range(0, PACK, step):
+                part = slice(t0, t0 + step)
+                nc.scalar.activation(
+                    term[:, part, :], y[:, part, :], ACT.Copy, scale=gcol[:, h, d : d + 1]
+                )
             return term
 
         def gated_plus(d, h, other, tag, step):
@@ -150,16 +148,21 @@ def tile_picked_zbloom_gelu_po_kernel(
                 )
             return term
 
-        a0 = gated_on_scalar(0, 0, "a0")
-        b0 = gated_on_scalar(1, 0, "b0")
-        c0 = gated_plus(2, 0, a0, "c0", PACK)
-        a1 = gated_on_scalar(0, 1, "a1")
-        d0 = gated_plus(3, 0, b0, "d0", PACK)
-        b1 = gated_on_scalar(1, 1, "b1")
-        c1 = gated_plus(2, 1, a1, "c1", PACK)
-        d1 = gated_plus(3, 1, b1, "d1", PACK // 2)
+        a0 = gated_on_scalar(0, 0, "a0", PACK)
+        a1 = gated_on_scalar(0, 1, "a1", PACK)
+        b0 = gated_plus(1, 0, a0, "b0", PACK)
+        b1 = gated_plus(1, 1, a1, "b1", PACK)
+        c0 = gated_plus(2, 0, b0, "c0", PACK)
+        d0 = gated_on_scalar(3, 0, "d0", PACK)
+        c1 = gated_plus(2, 1, b1, "c1", PACK)
+        d1 = gated_on_scalar(3, 1, "d1", PACK // 2)
         terms = [[c0, d0], [c1, d1]]
 
+        w2_codes = keep.tile([P, N], U32, name="w2_codes", align_bytes=64)
+        nc.scalar.copy(
+            w2_codes[:].rearrange("p (t m) -> p m t", t=PACK),
+            w2w_raw[:].rearrange("p (m t) -> p m t", t=PACK),
+        )
         w2_plane = keep.tile([P, N], U8, name="w2_plane", align_bytes=64, tag="b1")
         nc.vector.tensor_copy(
             w2_plane[:].rearrange("p (t m) -> p t m", t=PACK),
@@ -190,7 +193,7 @@ def tile_picked_zbloom_gelu_po_kernel(
         for lo, hi in PIECES:
             width = hi - lo
             u = sums[lo // P]
-            z_bf = keep.tile([P, width * PACK], BF16, name="z_bf%d" % lo, align_bytes=64)
+            z_bf = keep.tile([P, width * PACK], BF16, name="z_bf%d" % lo, align_bytes=64, tag="bf%d" % lo)
             nc.scalar.activation(
                 z_bf[:].rearrange("p (v t) -> p v t", t=PACK),
                 u[:, :, lo % P : lo % P + width].rearrange("p t v -> p v t"),
@@ -215,19 +218,22 @@ def tile_picked_zbloom_gelu_po_kernel(
                     start=True,
                     stop=True,
                 )
-            o_bf = keep.tile([P, width * PACK], BF16, name="o_bf%d" % lo, align_bytes=64)
+            o_bf = keep.tile([P, width * PACK], BF16, name="o_bf%d" % lo, align_bytes=64, tag="bf%d" % (P - lo))
             nc.vector.tensor_copy(
                 o_bf[:].rearrange("p (v t) -> p v t", t=PACK), o[:].rearrange("p t v -> p v t")
             )
             o_f32 = keep.tile([P, PACK, width], F32, name="o_f32%d" % lo)
-            nc.scalar.copy(o_f32[:], o[:])
-            queue = nc.scalar if hi == V else nc.sync
-            queue.dma_start(out_rows[:, :, cols], o_f32[:])
+            step = PACK // 2 if hi == V else PACK
+            for t0 in range(0, PACK, step):
+                part = slice(t0, t0 + step)
+                nc.scalar.copy(o_f32[:, part, :], o[:, part, :])
+                queue = nc.scalar if hi == V and t0 > 0 else nc.sync
+                queue.dma_start(out_rows[:, part, cols], o_f32[:, part, :])
             nc.vector.quantize_mx(
                 out=out_codes[:, cols].bitcast(FP8X4), scales=out_plane[:, cols], in_=o_bf[:]
             )
+            nc.sync.dma_start(out_words[:, cols], out_codes[:, cols].bitcast(I32))
 
-        nc.sync.dma_start(out_words, out_codes[:].bitcast(I32))
         for q in range(4):
             queue = nc.scalar if q % 2 == 0 else nc.sync
             queue.dma_start(

from contextlib import ExitStack

import concourse.mybir as mybir
from concourse.masks import make_identity

K, T, S, D, V, H, N = 512, 4096, 1024, 4, 256, 512, 512
FLOPS = 2 * K * H * S + 2 * H * N * V

F32 = mybir.dt.float32
BF16 = mybir.dt.bfloat16
I32 = mybir.dt.int32
U32 = mybir.dt.uint32
U16 = mybir.dt.uint16
U8 = mybir.dt.uint8
FP8X4 = mybir.dt.float8_e4m3fn_x4
ACT = mybir.ActivationFunctionType
ALU = mybir.AluOpType

P = 128
PACK = 4
HALVES = V // P
SCALE_ROWS = 16
PIECES = ((0, 128), (128, 256))
ORDER = ((0, 0), (0, 1), (1, 0), (1, 1), (2, 0), (3, 0), (2, 1), (3, 1))
STAGE_ROW = P - SCALE_ROWS


def tile_picked_zbloom_gelu_po_kernel(
    tc, x_words, x_scales, w1, w2_words, w2_scales, gate, offs, out_0, out_1, out_2
):
    nc = tc.nc
    with ExitStack() as ctx:
        keep = ctx.enter_context(tc.tile_pool(name="keep", bufs=1))
        psum = ctx.enter_context(tc.psum_pool(name="psum", bufs=1))

        offsets = keep.tile([P, S // 16], U16, name="offsets")
        nc.sync.dma_start(offsets[:], offs)

        xs_table = keep.tile([P, T], U8, name="xs_table", align_bytes=64)
        nc.scalar.dma_start(
            xs_table[STAGE_ROW : STAGE_ROW + SCALE_ROWS, :].bitcast(I32), x_scales[0].bitcast(I32)
        )
        nc.vector.memset(xs_table[0:STAGE_ROW, :].bitcast(I32), 0)

        gate_rows = keep.tile([P, V], F32, name="gate_rows")
        nc.scalar.dma_start(gate_rows[P - D : P, :], gate[:, 0, :])
        nc.vector.memset(gate_rows[0 : P - D, :], 0.0)

        w1_raw = keep.tile([P, PACK, H], F32, name="w1_raw", align_bytes=64, tag="w1_raw")
        nc.sync.dma_start(w1_raw[:], w1.rearrange("(p j) c -> p j c", j=PACK))

        xw_table = keep.tile([P, T], U32, name="xw_table", align_bytes=64)
        nc.sync.dma_start(
            xw_table[:].bitcast(I32),
            x_words[0].rearrange("p c r -> p (c r)").bitcast(I32),
        )

        w2w_raw = keep.tile([P, N], U32, name="w2w_raw", align_bytes=64)
        nc.sync.dma_start(
            w2w_raw[:].bitcast(I32), w2_words[0].rearrange("p c r -> p (c r)").bitcast(I32)
        )

        ident = keep.tile([P, P], F32, name="ident")
        make_identity(nc, ident[:])

        xs_plane = keep.tile([P, S], U8, name="xs_plane", align_bytes=64)
        nc.vector.memset(xs_plane[:].bitcast(I32), 0)

        seed = keep.tile([P, 1], F32, name="seed")
        nc.vector.memset(seed[:], 0.0)
        unread = keep.tile([P, 1], F32, name="unread")
        nc.scalar.activation(unread[:], seed[:], ACT.Gelu_apprx_tanh)

        gate_t = psum.tile([P, HALVES, P], F32, name="gate_t", tag="bank7")
        for h in range(HALVES):
            nc.tensor.transpose(gate_t[:, h, :], gate_rows[:, h * P : (h + 1) * P], ident[:])
        gcol = keep.tile([P, HALVES, D], F32, name="gcol")
        nc.scalar.copy(gcol[:], gate_t[:, :, P - D : P])

        xs_picked = keep.tile([P, S], U8, name="xs_picked", align_bytes=64)
        nc.vector.tensor_copy(xs_picked[:], xs_table[:].indirect(offsets[:]))
        for q in range(4):
            nc.scalar.dma_start(
                xs_plane[32 * q : 32 * q + 4, :].bitcast(I32),
                xs_picked[STAGE_ROW + 4 * q : STAGE_ROW + 4 * q + 4, :].bitcast(I32),
            )

        w1_bf = keep.tile([P, PACK * H], BF16, name="w1_bf", align_bytes=64)
        nc.vector.tensor_copy(
            w1_bf[:].rearrange("p (c j) -> p c j", j=PACK),
            w1_raw[:].rearrange("p j c -> p c j"),
        )
        w1_codes = keep.tile([P, H], U32, name="w1_codes", align_bytes=64)
        w1_plane = keep.tile([P, H], U8, name="w1_plane", align_bytes=64)
        nc.vector.quantize_mx(out=w1_codes[:].bitcast(FP8X4), scales=w1_plane[:], in_=w1_bf[:])

        w2s_raw = keep.tile([P, N], U8, name="w2s_raw", align_bytes=64, tag="w1_raw")
        nc.vector.memset(w2s_raw[:].bitcast(I32), 0)
        for q in range(4):
            nc.sync.dma_start(
                w2s_raw[32 * q : 32 * q + 4, :].bitcast(I32),
                w2_scales[0, 4 * q : 4 * q + 4, :].bitcast(I32),
            )

        xw_picked = []
        for d in range(D):
            picked = keep.tile([P, V], U32, name="xw_picked%d" % d, align_bytes=64)
            nc.vector.tensor_copy(
                picked[:], xw_table[:].indirect(offsets[:, d * V // 16 : (d + 1) * V // 16])
            )
            xw_picked.append(picked)

        def product(d, h):
            y = psum.tile([P, H], F32, name="y%d%d" % (d, h), tag="bank%d" % (ORDER.index((d, h)) % 6))
            nc.tensor.matmul_mx(
                out=y[:],
                lhsT=xw_picked[d][:, h * P : (h + 1) * P].bitcast(FP8X4),
                lhsT_scale=xs_plane[:, d * V + h * P : d * V + (h + 1) * P],
                rhs=w1_codes[:].bitcast(FP8X4),
                rhs_scale=w1_plane[:],
                start=True,
                stop=True,
            )
            return y[:].rearrange("p (m t) -> p t m", t=PACK)

        def gated_on_scalar(d, h, tag, step):
            y = product(d, h)
            term = keep.tile([P, PACK, P], F32, name="term%d%d" % (d, h), tag=tag, align_bytes=64)
            for t0 in range(0, PACK, step):
                part = slice(t0, t0 + step)
                nc.scalar.activation(
                    term[:, part, :], y[:, part, :], ACT.Copy, scale=gcol[:, h, d : d + 1]
                )
            return term

        def gated_plus(d, h, other, tag, step):
            y = product(d, h)
            term = keep.tile([P, PACK, P], F32, name="term%d%d" % (d, h), tag=tag, align_bytes=64)
            for t0 in range(0, PACK, step):
                part = slice(t0, t0 + step)
                nc.vector.scalar_tensor_tensor(
                    term[:, part, :],
                    y[:, part, :],
                    gcol[:, h, d : d + 1],
                    other[:, part, :],
                    ALU.mult,
                    ALU.add,
                )
            return term

        a0 = gated_on_scalar(0, 0, "a0", PACK)
        a1 = gated_on_scalar(0, 1, "a1", PACK)
        b0 = gated_plus(1, 0, a0, "b0", PACK)
        b1 = gated_plus(1, 1, a1, "b1", PACK)
        c0 = gated_plus(2, 0, b0, "c0", PACK)
        d0 = gated_on_scalar(3, 0, "d0", PACK)
        c1 = gated_plus(2, 1, b1, "c1", PACK)
        d1 = gated_on_scalar(3, 1, "d1", PACK // 2)
        terms = [[c0, d0], [c1, d1]]

        w2_codes = keep.tile([P, N], U32, name="w2_codes", align_bytes=64)
        nc.scalar.copy(
            w2_codes[:].rearrange("p (t m) -> p m t", t=PACK),
            w2w_raw[:].rearrange("p (m t) -> p m t", t=PACK),
        )
        w2_plane = keep.tile([P, N], U8, name="w2_plane", align_bytes=64, tag="b1")
        nc.vector.tensor_copy(
            w2_plane[:].rearrange("p (t m) -> p t m", t=PACK),
            w2s_raw[:].rearrange("p (m t) -> p t m", t=PACK),
        )

        out_codes = keep.tile([P, V], U32, name="out_codes", align_bytes=64)
        out_plane = keep.tile([P, V], U8, name="out_plane", align_bytes=64)
        out_rows = out_0.rearrange("(p t) v -> p t v", t=PACK)
        out_words = out_1[0].rearrange("p c r -> p (c r)").bitcast(I32)

        sums = []
        for h in range(HALVES):
            u = psum.tile([P, PACK, P], F32, name="u%d" % h, tag="bank%d" % (6 + h))
            steps = [(term, t) for term in terms[h] for t in range(PACK)]
            for n, (term, t) in enumerate(steps):
                nc.tensor.matmul(
                    u[:, t, :],
                    term[:, t, :],
                    ident[:],
                    start=(n == 0),
                    stop=(n == len(steps) - 1),
                    is_transpose=True,
                )
            sums.append(u)

        z_ops = []
        for lo, hi in PIECES:
            width = hi - lo
            u = sums[lo // P]
            z_bf = keep.tile([P, width * PACK], BF16, name="z_bf%d" % lo, align_bytes=64, tag="bf%d" % lo)
            nc.scalar.activation(
                z_bf[:].rearrange("p (v t) -> p v t", t=PACK),
                u[:, :, lo % P : lo % P + width].rearrange("p t v -> p v t"),
                ACT.Gelu_apprx_tanh,
            )
            z_codes = keep.tile([P, width], U32, name="z_codes%d" % lo, align_bytes=64)
            z_plane = keep.tile([P, width], U8, name="z_plane%d" % lo, align_bytes=64)
            nc.vector.quantize_mx(out=z_codes[:].bitcast(FP8X4), scales=z_plane[:], in_=z_bf[:])
            z_ops.append((z_codes, z_plane))

        for n, ((lo, hi), (z_codes, z_plane)) in enumerate(zip(PIECES, z_ops)):
            width = hi - lo
            cols = slice(lo, hi)
            o = psum.tile([P, PACK, width], F32, name="o%d" % lo, tag="bank%d" % (1 + n))
            for t in range(PACK):
                nc.tensor.matmul_mx(
                    out=o[:, t, :],
                    lhsT=w2_codes[:, t * P : (t + 1) * P].bitcast(FP8X4),
                    lhsT_scale=w2_plane[:, t * P : (t + 1) * P],
                    rhs=z_codes[:].bitcast(FP8X4),
                    rhs_scale=z_plane[:],
                    start=True,
                    stop=True,
                )
            o_bf = keep.tile([P, width * PACK], BF16, name="o_bf%d" % lo, align_bytes=64, tag="bf%d" % (P - lo))
            nc.vector.tensor_copy(
                o_bf[:].rearrange("p (v t) -> p v t", t=PACK), o[:].rearrange("p t v -> p v t")
            )
            o_f32 = keep.tile([P, PACK, width], F32, name="o_f32%d" % lo)
            step = PACK // 2 if hi == V else PACK
            for t0 in range(0, PACK, step):
                part = slice(t0, t0 + step)
                nc.scalar.copy(o_f32[:, part, :], o[:, part, :])
                queue = nc.scalar if hi == V and t0 > 0 else nc.sync
                queue.dma_start(out_rows[:, part, cols], o_f32[:, part, :])
            nc.vector.quantize_mx(
                out=out_codes[:, cols].bitcast(FP8X4), scales=out_plane[:, cols], in_=o_bf[:]
            )
            nc.sync.dma_start(out_words[:, cols], out_codes[:, cols].bitcast(I32))

        for q in range(4):
            queue = nc.scalar if q % 2 == 0 else nc.sync
            queue.dma_start(
                out_2[0, 4 * q : 4 * q + 4, :].bitcast(I32),
                out_plane[32 * q : 32 * q + 4, :].bitcast(I32),
            )
